import numpy as np
import ml_dtypes

BF16 = ml_dtypes.bfloat16


def bf(x):
    return np.asarray(x, np.float32).astype(BF16)


def f32(x):
    return np.asarray(x, np.float32)


def f64(x):
    return np.asarray(x).astype(np.float64)


def striped(idx):
    return np.tile(idx.reshape(-1, 16).T, (8, 1))


S, K, M, N = 256, 128, 256, 64


def gelu_tanh(v):
    return 0.5 * v * (1.0 + np.tanh(np.sqrt(2.0 / np.pi) * (v + 0.044715 * v**3)))


def setup_inputs():
    return {"base": bf(np.random.standard_normal((M, S))), "x": bf(np.random.standard_normal((K, N))), "w": bf(np.random.standard_normal((K, M)) / np.sqrt(K)), "b": f32(0.5 * np.random.standard_normal((M, 1))), "offs": striped(np.random.permutation(S)[:N])}


def reference(base, x, w, b, offs):
    idx = offs[:16].T.reshape(-1)
    z = f64(base).copy()
    z[:, idx] = f64(w).T @ f64(x)
    return gelu_tanh(z + f64(b))

@@ -1,0 +1,48 @@
+import concourse.mybir as mybir
+from concourse.masks import make_identity
+
+BF16, F32, U16 = mybir.dt.bfloat16, mybir.dt.float32, mybir.dt.uint16
+GELU = mybir.ActivationFunctionType.Gelu_apprx_tanh
+
+P = 128
+M, S, K, N = 256, 256, 128, 64
+BLOCKS = M // P
+
+FLOPS = 2 * M * K * N
+
+
+def tile_scatter_matmul_kernel(tc, base, x, w, b, offs, out):
+    nc = tc.nc
+    with (
+        tc.tile_pool(name="held", bufs=1) as held,
+        tc.psum_pool(name="psum", bufs=1) as psum,
+    ):
+        base_tile = held.tile([P, BLOCKS, S], BF16, name="base_tile")
+        offsets = held.tile([P, N // 16], U16, name="offsets")
+        weights = held.tile([P, M], BF16, name="weights")
+        moving = held.tile([P, N], BF16, name="moving")
+        bias = held.tile([P, BLOCKS], F32, name="bias")
+        ident = held.tile([P, P], BF16, name="ident")
+
+        nc.sync.dma_start(base_tile[:], base.rearrange("(a p) s -> p a s", p=P))
+        nc.sync.dma_start(weights[:], w)
+        nc.sync.dma_start(moving[:], x)
+        nc.sync.dma_start(offsets[:], offs)
+        nc.scalar.dma_start(bias[:], b.rearrange("(a p) o -> p (a o)", p=P))
+
+        make_identity(nc, ident[:])
+
+        windows = [psum.tile([P, S], F32, name=f"window{a}") for a in range(BLOCKS)]
+
+        for a in range(BLOCKS):
+            nc.tensor.matmul(windows[a][:], ident[:], base_tile[:, a, :], start=True, stop=True)
+
+        for a in range(BLOCKS):
+            nc.tensor.matmul(
+                windows[a][:].indirect(offsets[:]), weights[:, a * P : (a + 1) * P], moving[:], start=True, stop=True
+            )
+
+        for a in range(BLOCKS):
+            result = held.tile([P, S], F32, name=f"result{a}")
+            nc.scalar.activation(result[:], windows[a][:], GELU, bias=bias[:, a : a + 1])
+            nc.sync.dma_start(out[a * P : (a + 1) * P, :], result[:])

@@ -13,6 +13,7 @@ FLOPS = 2 * M * K * N
 
 def tile_scatter_matmul_kernel(tc, base, x, w, b, offs, out):
     nc = tc.nc
+    out_rows = out.rearrange("(p a) s -> p a s", p=P)
     with (
         tc.tile_pool(name="held", bufs=1) as held,
         tc.psum_pool(name="psum", bufs=1) as psum,
@@ -24,11 +25,16 @@ def tile_scatter_matmul_kernel(tc, base, x, w, b, offs, out):
         bias = held.tile([P, BLOCKS], F32, name="bias")
         ident = held.tile([P, P], BF16, name="ident")
 
-        nc.sync.dma_start(base_tile[:], base.rearrange("(a p) s -> p a s", p=P))
+        nc.sync.dma_start(base_tile[:], base.rearrange("(p a) s -> p a s", p=P))
         nc.sync.dma_start(weights[:], w)
         nc.sync.dma_start(moving[:], x)
         nc.sync.dma_start(offsets[:], offs)
-        nc.scalar.dma_start(bias[:], b.rearrange("(a p) o -> p (a o)", p=P))
+        nc.scalar.dma_start(bias[:], b.rearrange("(p a) o -> p (a o)", p=P))
+
+        zeros = held.tile([P, 1], F32, name="zeros")
+        table_call = held.tile([P, 1], F32, name="table_call")
+        nc.vector.memset(zeros[:], 0.0)
+        nc.scalar.activation(table_call[:], zeros[:], GELU)
 
         make_identity(nc, ident[:])
 
@@ -39,10 +45,10 @@ def tile_scatter_matmul_kernel(tc, base, x, w, b, offs, out):
 
         for a in range(BLOCKS):
             nc.tensor.matmul(
-                windows[a][:].indirect(offsets[:]), weights[:, a * P : (a + 1) * P], moving[:], start=True, stop=True
+                windows[a][:].indirect(offsets[:]), weights[:, a::BLOCKS], moving[:], start=True, stop=True
             )
 
         for a in range(BLOCKS):
             result = held.tile([P, S], F32, name=f"result{a}")
             nc.scalar.activation(result[:], windows[a][:], GELU, bias=bias[:, a : a + 1])
-            nc.sync.dma_start(out[a * P : (a + 1) * P, :], result[:])
+            nc.sync.dma_start(out_rows[:, a, :], result[:])

@@ -8,6 +8,9 @@ P = 128
 M, S, K, N = 256, 256, 128, 64
 BLOCKS = M // P
 
+WARM_COLUMNS = 512
+WARM_MATMULS = 4
+
 FLOPS = 2 * M * K * N
 
 
@@ -37,6 +40,12 @@ def tile_scatter_matmul_kernel(tc, base, x, w, b, offs, out):
         nc.scalar.activation(table_call[:], zeros[:], GELU)
 
         make_identity(nc, ident[:])
+
+        warm_moving = held.tile([P, WARM_COLUMNS], BF16, name="warm_moving")
+        warm_bank = psum.tile([P, WARM_COLUMNS], F32, name="warm_bank")
+        nc.vector.memset(warm_moving[:], 0.0)
+        for repeat in range(WARM_MATMULS):
+            nc.tensor.matmul(warm_bank[:], warm_moving[:, :P], warm_moving[:], start=True, stop=True)
 
         windows = [psum.tile([P, S], F32, name=f"window{a}") for a in range(BLOCKS)]
 

@@ -8,8 +8,8 @@ P = 128
 M, S, K, N = 256, 256, 128, 64
 BLOCKS = M // P
 
-WARM_COLUMNS = 512
-WARM_MATMULS = 4
+WARM_COLUMNS = S
+WARM_MATMULS = 5
 
 FLOPS = 2 * M * K * N
 
@@ -32,7 +32,7 @@ def tile_scatter_matmul_kernel(tc, base, x, w, b, offs, out):
         nc.sync.dma_start(weights[:], w)
         nc.sync.dma_start(moving[:], x)
         nc.sync.dma_start(offsets[:], offs)
-        nc.scalar.dma_start(bias[:], b.rearrange("(p a) o -> p (a o)", p=P))
+        nc.sync.dma_start(bias[:], b.rearrange("(p a) o -> p (a o)", p=P))
 
         zeros = held.tile([P, 1], F32, name="zeros")
         table_call = held.tile([P, 1], F32, name="table_call")
@@ -57,7 +57,8 @@ def tile_scatter_matmul_kernel(tc, base, x, w, b, offs, out):
                 windows[a][:].indirect(offsets[:]), weights[:, a::BLOCKS], moving[:], start=True, stop=True
             )
 
+        store_queues = (nc.sync, nc.scalar)
         for a in range(BLOCKS):
             result = held.tile([P, S], F32, name=f"result{a}")
             nc.scalar.activation(result[:], windows[a][:], GELU, bias=bias[:, a : a + 1])
-            nc.sync.dma_start(out_rows[:, a, :], result[:])
+            store_queues[a % 2].dma_start(out_rows[:, a, :], result[:])

import concourse.mybir as mybir
from concourse.masks import make_identity

BF16, F32, U16 = mybir.dt.bfloat16, mybir.dt.float32, mybir.dt.uint16
GELU = mybir.ActivationFunctionType.Gelu_apprx_tanh

P = 128
M, S, K, N = 256, 256, 128, 64
BLOCKS = M // P

WARM_COLUMNS = S
WARM_MATMULS = 5

FLOPS = 2 * M * K * N


def tile_scatter_matmul_kernel(tc, base, x, w, b, offs, out):
    nc = tc.nc
    out_rows = out.rearrange("(p a) s -> p a s", p=P)
    with (
        tc.tile_pool(name="held", bufs=1) as held,
        tc.psum_pool(name="psum", bufs=1) as psum,
    ):
        base_tile = held.tile([P, BLOCKS, S], BF16, name="base_tile")
        offsets = held.tile([P, N // 16], U16, name="offsets")
        weights = held.tile([P, M], BF16, name="weights")
        moving = held.tile([P, N], BF16, name="moving")
        bias = held.tile([P, BLOCKS], F32, name="bias")
        ident = held.tile([P, P], BF16, name="ident")

        nc.sync.dma_start(base_tile[:], base.rearrange("(p a) s -> p a s", p=P))
        nc.sync.dma_start(weights[:], w)
        nc.sync.dma_start(moving[:], x)
        nc.sync.dma_start(offsets[:], offs)
        nc.sync.dma_start(bias[:], b.rearrange("(p a) o -> p (a o)", p=P))

        zeros = held.tile([P, 1], F32, name="zeros")
        table_call = held.tile([P, 1], F32, name="table_call")
        nc.vector.memset(zeros[:], 0.0)
        nc.scalar.activation(table_call[:], zeros[:], GELU)

        make_identity(nc, ident[:])

        warm_moving = held.tile([P, WARM_COLUMNS], BF16, name="warm_moving")
        warm_bank = psum.tile([P, WARM_COLUMNS], F32, name="warm_bank")
        nc.vector.memset(warm_moving[:], 0.0)
        for repeat in range(WARM_MATMULS):
            nc.tensor.matmul(warm_bank[:], warm_moving[:, :P], warm_moving[:], start=True, stop=True)

        windows = [psum.tile([P, S], F32, name=f"window{a}") for a in range(BLOCKS)]

        for a in range(BLOCKS):
            nc.tensor.matmul(windows[a][:], ident[:], base_tile[:, a, :], start=True, stop=True)

        for a in range(BLOCKS):
            nc.tensor.matmul(
                windows[a][:].indirect(offsets[:]), weights[:, a::BLOCKS], moving[:], start=True, stop=True
            )

        store_queues = (nc.sync, nc.scalar)
        for a in range(BLOCKS):
            result = held.tile([P, S], F32, name=f"result{a}")
            nc.scalar.activation(result[:], windows[a][:], GELU, bias=bias[:, a : a + 1])
            store_queues[a % 2].dma_start(out_rows[:, a, :], result[:])
